import numpy as np, ml_dtypes
CORES = [1,2,5,7,57,58,61,63,73,74,77,79]
N = 12
import mx_ref
NC, G = 128, 4
C = np.float32(0.029)
BF = ml_dtypes.bfloat16
def tile(rs):
    return np.stack(rs, axis=2).reshape(128, -1).astype(BF)
def act(Z):
    return [np.maximum(z, 0) * C for z in Z]
def pk(c, s, i=0):
    return (np.ascontiguousarray(c[:, 512 * i:512 * i + 512]), mx_ref.live(s[:, 128 * i:128 * i + 128]))
def inputs(rng, e, E):
    def f(*shape):
        v = (rng.standard_normal(shape, dtype=np.float32) * np.exp2(rng.integers(-2, 3, shape[:-1] + (1,)))).astype(BF)
        return mx_ref.spread((v.astype(np.float32) * np.exp2(rng.integers(-E, E + 1, shape[:-2] + (1, 1))).astype(np.float32)).astype(BF), rng, e)
    def packed(k):
        c = np.zeros((N, 128, k * 512), np.uint8); s = np.zeros((N, 128, k * 128), np.uint8)
        for r in range(N):
            for i in range(k):
                a, b = mx_ref.quantize(f(128, 512)); c[r][:, 512 * i:512 * i + 512] = a; s[r][:, 128 * i:128 * i + 128] = mx_ref.plane(b, rng)
        return c, s
    d = {}
    d["ac"], d["az"] = packed(1)
    d["bc"], d["bs"] = packed(1)
    d["cc"], d["cs"] = packed(1)
    d["x"] = f(N, 128, 4 * NC)
    return d
def setup_inputs(rng):
    return inputs(rng, 0, 0)
def setup_inputs_blocks(rng):
    return inputs(rng, 2, 0)
def setup_inputs_wide(rng):
    return inputs(rng, 0, 4)
def reference(ac, az, bc, bs, cc, cs, x):
    y = np.zeros((N, 128, N * NC), np.float32)
    for r in range(N):
        h = mx_ref.quantize(tile(act([mx_ref.matmul(pk(ac[i], az[i]), mx_ref.quantize(x[r])) for i in range(G)])))
        h = mx_ref.quantize(tile(act([mx_ref.matmul(pk(bc[i], bs[i]), h) for i in range(G)])))
        for j in range(N):
            y[r][:, NC * j:NC * j + NC] = mx_ref.matmul(pk(cc[j], cs[j]), h)
    return {"y": y}

@@ -1,0 +1,408 @@
+import numpy
+from concourse.bass import DstId, RemoteDMATransfer
+from concourse.mybir import dt, AluOpType, ActivationFunctionType
+
+NC, G, NR, SIM = 128, 4, 12, 80
+SCALE = float(numpy.float32(0.029))
+X4 = "float8_e4m3fn_x4"
+
+SCRATCH = {
+    "tx": ("sbuf", [128, G * NC], "bfloat16"),
+    "tg": ("sbuf", [128, G * NC], "bfloat16"),
+    "qa": ("sbuf", [128, 2 * NC], X4), "qap": ("sbuf", [128, 2 * NC], "uint8"),
+    "qb": ("sbuf", [128, NC], X4), "qbp": ("sbuf", [128, NC], "uint8"),
+    "w": ("sbuf", [128, 2 * NC], X4), "wp": ("sbuf", [128, 2 * NC], "uint8"),
+    "wc": ("sbuf", [128, 3 * NC], X4), "wcp": ("sbuf", [128, 3 * NC], "uint8"),
+    "yb": ("sbuf", [128, 3 * NC], "float32"),
+    "ps": ("psum", [128, 8 * 512], "float32"),
+    "dG": ("dram", [128, NC], X4), "dH": ("dram", [128, NC], "uint8"),
+    "dX": ("dram", [128, NC], X4), "dY": ("dram", [128, NC], "uint8"),
+}
+SEMAPHORES = ["iA", "iZ", "iB", "iT", "iC", "ix", "ls", "lsC", "lsG", "vq", "v1", "v2", "lG",
+              "rQ", "rR", "rG", "rH", "rDG", "rDH", "rh", "ri"]
+for _i in range(G):
+    for _n, _t, _d in (("dA%d", X4, NC), ("dZ%d", "uint8", NC), ("dB%d", X4, NC), ("dT%d", "uint8", NC)):
+        SCRATCH[_n % _i] = ("dram", [128, _d], _t)
+    SEMAPHORES += [s % _i for s in ("rA%d", "rZ%d", "rB%d", "rT%d", "rC%d", "rP%d", "lW%d", "lV%d", "mP%d", "mQ%d", "aP%d", "aQ%d",
+                                    "mD%d", "mE%d", "mS%d", "cD%d", "cE%d", "cS%d", "lD%d", "lS%d", "sD%d", "sS%d")]
+for _c in range(3):
+    for _i in range(2):
+        SCRATCH["dW%d%d" % (_c, _i)] = ("dram", [128, 2 * NC], X4)
+        SCRATCH["dV%d%d" % (_c, _i)] = ("dram", [128, 2 * NC], "uint8")
+        SEMAPHORES += ["rW%d%d" % (_c, _i), "rV%d%d" % (_c, _i)]
+PLANES = ("wp", "wcp", "qap", "qbp", "dH", "dY")
+
+
+def bits(mask):
+    return [b for b in range(16) if mask >> b & 1]
+
+
+def part(mask, k, n):
+    b = bits(mask)
+    m = len(b) // n
+    return sum(1 << e for e in b[k * m:k * m + m])
+
+
+def layout(T, topo):
+    cores = list(T.cores)
+    chips = []
+    for c in cores:
+        if topo.chip(c) not in chips:
+            chips.append(topo.chip(c))
+    L = {"chips": chips, "ranks": [[c for c in cores if topo.chip(c) == ch] for ch in chips], "cores": cores}
+    far = lambda c: [s for s in cores if topo.chip(s) != topo.chip(c)]
+    owns = lambda c: all(topo.may_write(c, s) for s in far(c))
+    idle = [[c for c in range(SIM) if topo.chip(c) == ch and c not in cores] for ch in chips]
+    L["port"] = [[c for c in m if owns(c)] for m in L["ranks"]]
+    L["inner"] = [[c for c in m if not owns(c)] for m in L["ranks"]]
+    L["gather"] = [[c for c in m if owns(c)] for m in idle]
+    L["scatter"] = [[c for c in m if not owns(c)] for m in idle]
+    L["home"] = chips.index(topo.chip(cores[0]))
+    L["away"] = [k for k in range(len(chips)) if k != L["home"]]
+    L["pair"] = {}
+    for p, n in zip(L["port"], L["inner"]):
+        for c in p:
+            d = [v for v in n if topo.die(v) == topo.die(c)][0]
+            L["pair"][c], L["pair"][d] = d, c
+    return L
+
+
+def plan(L, topo):
+    prog = {}
+    home, away, chips = L["home"], L["away"], L["chips"]
+    rank = lambda c: L["cores"].index(c)
+    where = lambda c: chips.index(topo.chip(c))
+
+    def wait(c, *sems):
+        prog.setdefault(c, []).extend(("wait", s) for s in sems)
+
+    def send(c, ts, local="ls"):
+        prog.setdefault(c, []).append(("send", ts, local))
+
+    def onchip(c):
+        return topo.mask(c, [s for s in L["ranks"][where(c)] if s != c][0])
+
+    def offchip(c):
+        return topo.mask(c, L["ranks"][away[0] if where(c) == home else home][0])
+
+    def piece(kind, i, dsts, mask):
+        name = "d%s%s" % (kind, i)
+        return (name, None, [(d, name, None) for d in dsts], mask, "r%s%s" % (kind, i))
+
+    def c_out(c):
+        m = L["ranks"][where(c)]
+        k, rest = m.index(c), [s for s in m if s != c]
+        col = lambda n: (n * NC, n * NC + NC)
+        keep = (L["gather"][where(c)][k // 2], k % 2)
+        wait(c, "iC")
+        for buf, last, r in (("wc", "dX", "rC%d"), ("wcp", "dY", "rP%d")):
+            if k < 3:
+                ts = [(buf, col(k), [(s, buf, col(k)) for s in rest] + [(keep[0], buf, col(keep[1]))], onchip(c), r % k)]
+            else:
+                ts = [(last, None, [(s, last, None) for s in rest], part(onchip(c), 1, 2), r % k),
+                      (last, None, [(keep[0], buf, col(keep[1]))], part(onchip(c), 0, 2), r % k)]
+            send(c, ts, "lsC")
+
+    def pass_on(c, src, cols, dst, dcols, sems, local):
+        for s, d, r in zip(src, dst, sems):
+            send(c, [(s, cols, [(L["pair"][c], d, dcols)], onchip(c), r)], local)
+
+    qx, qg = (0, NC), (NC, 2 * NC)
+    for k in range(len(chips)):
+        ports, inners = L["port"][k], L["inner"][k]
+        for c in inners:
+            i = rank(c)
+            if k == home:
+                e = L["pair"][c]
+                e2 = [s for s in ports if s != e][0]
+                l2 = [s for s in inners if s != c][0]
+                for kind, other in (("A", e2), ("Z", e2), ("B", l2), ("T", l2)):
+                    wait(c, "i" + kind)
+                    send(c, [piece(kind, i, [e], part(onchip(c), 0, 2)), piece(kind, i, [other], part(onchip(c), 1, 2))])
+            wait(c, "vq")
+            pass_on(c, ("qa", "qap"), qx, ("qa", "qap"), qg, ("rQ", "rR"), "ls")
+            c_out(c)
+            wait(c, "v1", "rDG", "rDH")
+            pass_on(c, ("qb", "qbp"), None, ("qb", "qbp"), None, ("rh", "ri"), "lsG")
+        for c in ports:
+            i = rank(c)
+            if k == home:
+                off = offchip(c)
+                on = onchip(c) & ~off
+                l = rank(L["pair"][c])
+                e2 = [s for s in ports if s != c]
+                wants_a = [s for v in away for s in L["port"][v]]
+                wants_b = [s for v in away for s in L["inner"][v]]
+                for kind in "AZ":
+                    wait(c, "i" + kind)
+                    send(c, [piece(kind, i, wants_a, off), piece(kind, i, e2, on)])
+                for kind in "AZ":
+                    wait(c, "r%s%d" % (kind, l))
+                    send(c, [piece(kind, l, wants_a, off)])
+                for kind in "BT":
+                    wait(c, "i" + kind, "r%s%d" % (kind, l))
+                    send(c, [piece(kind, i, wants_b, part(off, 0, 2)), piece(kind, l, wants_b, part(off, 1, 2)),
+                             piece(kind, i, inners, on)])
+            c_out(c)
+            wait(c, "v1")
+            pass_on(c, ("qb", "qbp"), None, ("qa", "qap"), qg, ("rG", "rH"), "lsG")
+            wait(c, "v2")
+            pass_on(c, ("qb", "qbp"), None, ("dG", "dH"), None, ("rDG", "rDH"), "ls")
+        for n in range(2):
+            c = L["gather"][k][n]
+            for buf, kind, r in (("wc", "W", "rC%d"), ("wcp", "V", "rP%d")):
+                name = "%s%d%d" % (kind, k, n)
+                wait(c, r % (2 * n), r % (2 * n + 1))
+                send(c, [(buf, (0, 2 * NC), [(L["scatter"][v][n], "d" + name, None) for v in range(len(chips)) if v != k],
+                          offchip(c), "r" + name)])
+            c = L["scatter"][k][n]
+            for v in near(L, topo, k):
+                for kind in "WV":
+                    name = "%d%d" % (v, n)
+                    wait(c, "r%s%s" % (kind, name))
+                    send(c, [piece(kind, name, L["ranks"][k], onchip(c))])
+    return prog
+
+
+def near(L, topo, k):
+    rest = [v for v in range(len(L["chips"])) if v != k]
+    return sorted(rest, key=lambda v: 0 if topo.same_plane(L["chips"][v], L["chips"][k]) else 1)
+
+
+def totals(prog, core):
+    n = {}
+    for c in prog:
+        for op in prog[c]:
+            if op[0] == "send":
+                for t in op[1]:
+                    e = len(bits(t[3]))
+                    for d in t[2]:
+                        if d[0] == core:
+                            n[t[4]] = n.get(t[4], 0) + e
+                    if c == core:
+                        n[op[2]] = n.get(op[2], 0) + e
+    return n
+
+
+def rank_program(g, core, T, topo):
+    L = layout(T, topo)
+    prog = plan(L, topo)
+    if core not in prog:
+        return
+    count = totals(prog, core)
+    for s in ("iA", "iZ", "iB", "iT", "ix"):
+        count[s] = 16
+    count["iC"] = 32
+    for s in ("vq", "v1", "v2"):
+        count[s] = 1
+    sem = T.sem
+
+    def wait(q, *names):
+        for n in names:
+            q.wait_ge(sem[n], count[n])
+
+    def view(name, cols):
+        t = T[name]
+        v = t[:, 0:t.shape[1]] if cols is None else t[:, cols[0]:cols[1]]
+        return v if name in PLANES or name[:2] in ("dZ", "dT", "dV") else v.bitcast(dt.uint8)
+
+    def copy(q, dst, dcols, src, scols, name):
+        q.dma_start(view(dst, dcols), view(src, scols)).then_inc(sem[name], 16)
+
+    def remote():
+        for op in prog[core]:
+            if op[0] == "wait":
+                wait(g, op[1])
+                continue
+            ts = []
+            for src, cols, dsts, mask, rsem in op[1]:
+                ids = []
+                for d in dsts:
+                    rid, pid, _s = topo.addr(d[0])
+                    ids.append(DstId(rid=rid, pnc=pid))
+                ts.append(RemoteDMATransfer(dst_ids=ids, dma_engine_mask=mask, remote_sem=sem[rsem], srcs=[view(src, cols)],
+                                            dsts=[view(d[1], d[2]) for d in dsts]))
+            g.remote_dma_fused(ts, local_sem=sem[op[2]])
+        if "ls" in count:
+            wait(g, "ls")
+
+    rank = T.rank_of(core)
+    if rank is None:
+        remote()
+        return
+    me = L["chips"].index(topo.chip(core))
+    mine = L["ranks"][me].index(core)
+    porty = core in L["port"][me]
+
+    if me != L["home"]:
+        g.sync.dma_start(T.tx[:], T.x[:]).then_inc(sem.ix, 16)
+    else:
+        g.sync.dma_start(view("dA%d" % rank, None), T.ac[:]).then_inc(sem.iA, 16)
+        g.scalar.dma_start(view("dZ%d" % rank, None), T.az[:]).then_inc(sem.iZ, 16)
+        g.sync.dma_start(T.tx[:], T.x[:]).then_inc(sem.ix, 16)
+        g.scalar.dma_start(view("dB%d" % rank, None), T.bc[:]).then_inc(sem.iB, 16)
+        g.sync.dma_start(view("dT%d" % rank, None), T.bs[:]).then_inc(sem.iT, 16)
+    slot = (mine * NC, mine * NC + NC)
+    own = (("wc", slot), ("wcp", slot)) if mine < 3 else (("dX", None), ("dY", None))
+    g.scalar.dma_start(view(own[0][0], own[0][1]), T.cc[:]).then_inc(sem.iC, 16)
+    g.sync.dma_start(view(own[1][0], own[1][1]), T.cs[:]).then_inc(sem.iC, 16)
+
+    remote()
+
+    order = [L["cores"].index(c) for c in L["port"][L["home"]] + L["inner"][L["home"]]]
+    kind = "AZ" if porty else "BT"
+
+    def load(q, k, name, after):
+        i, s = order[k], ((k % 2) * NC, (k % 2) * NC + NC)
+        h = "i" if i == rank else "r"
+        for x in kind:
+            wait(q, "i" + x if i == rank else "r%s%d" % (x, i))
+        if after:
+            q.wait_ge(sem[after], 1)
+        copy(q, "w", s, "d%s%d" % (kind[0], i), None, name)
+        copy(q, "wp", s, "d%s%d" % (kind[1], i), None, name)
+
+    def product(bank, w, s, q, cols, done):
+        n = cols[1] - cols[0]
+        g.tensor.matmul_mx(T.ps[:, 512 * bank:512 * bank + n], T[w][:, s * NC:s * NC + NC], T[w + "p"][:, s * NC:s * NC + NC],
+                           T[q][:, cols[0]:cols[1]], T[q + "p"][:, cols[0]:cols[1]], True, True).then_inc(sem[done], 1)
+
+    def step(k, col, m, a):
+        q = g.vector if k % 2 else g.scalar
+        q.wait_ge(sem[m % k], 1)
+        out, z = T.tg[:, order[k]:G * NC:G], T.ps[:, 512 * k + col:512 * k + col + NC]
+        if k % 2:
+            r = q.tensor_scalar(out, z, SCALE, 0.0, AluOpType.mult, AluOpType.max)
+        else:
+            r = q.activation(out, z, ActivationFunctionType.Relu, scale=SCALE)
+        r.then_inc(sem[a % k], 1)
+
+    def quantise(a, done):
+        for k in range(G):
+            g.vector.wait_ge(sem[a % k], 1)
+        if done == "v2":
+            wait(g.vector, "lsG")
+        g.vector.quantize_mx(T.qb[:, 0:NC], T.qbp[:, 0:NC], T.tg[:, 0:G * NC]).then_inc(sem[done], 1)
+
+    g.vector.wait_ge(sem.ix, 16)
+    g.vector.quantize_mx(T.qa[:, 0:NC], T.qap[:, 0:NC], T.tx[:, 0:G * NC]).then_inc(sem.vq, 1)
+    load(g.sync, 0, "lW0", None)
+    load(g.scalar, 1, "lW1", None)
+    if porty:
+        wait(g.tensor, "vq", "rQ", "rR")
+        for k in range(G):
+            g.tensor.wait_ge(sem["lW%d" % k], 32)
+            product(k, "w", k % 2, "qa", (0, 2 * NC), "mP%d" % k)
+        load(g.sync, 2, "lW2", "mP0")
+        step(0, 0, "mP%d", "aP%d")
+        load(g.scalar, 3, "lW3", "mP1")
+        for k in (1, 2, 3):
+            step(k, 0, "mP%d", "aP%d")
+        quantise("aP%d", "v1")
+        g.scalar.wait_ge(sem.v1, 1)
+        g.vector.wait_ge(sem.v1, 1)
+        for k in range(G):
+            step(k, NC, "mP%d", "aQ%d")
+        quantise("aQ%d", "v2")
+        wait(g.tensor, "rh", "ri")
+    else:
+        wait(g.tensor, "rG", "rH")
+        for k in range(G):
+            g.tensor.wait_ge(sem["lW%d" % k], 32)
+            product(k, "w", k % 2, "qa", (NC, 2 * NC), "mP%d" % k)
+        load(g.sync, 2, "lW2", "mP0")
+        load(g.scalar, 3, "lW3", "mP1")
+        for k in range(G):
+            step(k, 0, "mP%d", "aP%d")
+        quantise("aP%d", "v1")
+        wait(g.sync, "rDG", "rDH")
+        for k in range(G):
+            g.sync.wait_ge(sem["mP%d" % k], 1)
+        copy(g.sync, "qa", (NC, 2 * NC), "dG", None, "lG")
+        copy(g.sync, "qap", (NC, 2 * NC), "dH", None, "lG")
+        g.tensor.wait_ge(sem.lG, 32)
+        for k in (2, 3, 0, 1):
+            if k < 2:
+                g.tensor.wait_ge(sem["lV%d" % k], 32)
+            g.tensor.wait_ge(sem["aP%d" % k], 1)
+            product(k, "w", k % 2, "qa", (NC, 2 * NC), "mQ%d" % k)
+        load(g.sync, 0, "lV0", "mQ2")
+        load(g.scalar, 1, "lV1", "mQ3")
+        g.scalar.wait_ge(sem.v1, 1)
+        g.vector.wait_ge(sem.v1, 1)
+        for k in (2, 3, 0, 1):
+            step(k, 0, "mQ%d", "aQ%d")
+        quantise("aQ%d", "v2")
+        g.tensor.wait_ge(sem.v2, 1)
+
+    a, b = near(L, topo, me)
+    pairs = [(me, 0), (a, 0), (a, 1), (b, 0)]
+    singles = [(me, 2), (me, 3), (b, 2), (b, 3)]
+    first = lambda ch, i: L["cores"].index(L["ranks"][ch][i]) * NC
+    D, S = (0, 2 * NC), (2 * NC, 3 * NC)
+
+    def arrived(q, k, kinds):
+        if k == mine:
+            wait(q, "iC")
+        else:
+            wait(q, *[x % k for x in kinds])
+
+    for k in range(3):
+        arrived(g.tensor, k, ("rC%d", "rP%d"))
+    for r in range(4):
+        if r:
+            g.tensor.wait_ge(sem["lS%d" % r], 32)
+        if r >= 2:
+            g.tensor.wait_ge(sem["cS%d" % (r - 2)], 1)
+        product(6 + r % 2, "wc", 2, "qb", (0, NC), "mS%d" % r)
+        if r:
+            g.tensor.wait_ge(sem["lD%d" % r], 32)
+            g.tensor.wait_ge(sem["cD%d" % (r - 1)], 1)
+            g.tensor.wait_ge(sem["cE%d" % (r - 1)], 1)
+        product(4, "wc", 0, "qb", (0, NC), "mD%d" % r)
+        product(5, "wc", 1, "qb", (0, NC), "mE%d" % r)
+
+    for r in range(4):
+        if r == 0:
+            wait(g.sync, "lsC")
+        if r < 3:
+            n = "%d%d" % pairs[r + 1]
+            wait(g.sync, "rW" + n, "rV" + n)
+            g.sync.wait_ge(sem["mD%d" % r], 1)
+            g.sync.wait_ge(sem["mE%d" % r], 1)
+            copy(g.sync, "wc", D, "dW" + n, None, "lD%d" % (r + 1))
+            copy(g.sync, "wcp", D, "dV" + n, None, "lD%d" % (r + 1))
+        for n, m, c in ((0, "mD%d", "cD%d"), (1, "mE%d", "cE%d")):
+            g.vector.wait_ge(sem[m % r], 1)
+            if r:
+                g.vector.wait_ge(sem["sD%d" % (r - 1)], 16)
+            g.vector.tensor_copy(T.yb[:, n * NC:n * NC + NC], T.ps[:, 512 * (4 + n):512 * (4 + n) + NC]).then_inc(sem[c % r], 1)
+            g.sync.wait_ge(sem[c % r], 1)
+        j = first(pairs[r][0], 2 * pairs[r][1])
+        g.sync.dma_start(T.y[:, j:j + 2 * NC], T.yb[:, D[0]:D[1]]).then_inc(sem["sD%d" % r], 16)
+    for r in range(4):
+        q = g.scalar
+        if r == 0:
+            wait(q, "lsC")
+        q.wait_ge(sem["mS%d" % r], 1)
+        if r < 3:
+            if r == 0:
+                arrived(q, 3, ("rC%d", "rP%d"))
+                src = ("dX", "dY", None)
+            else:
+                n = "%d1" % b
+                wait(q, "rW" + n, "rV" + n)
+                src = ("dW" + n, "dV" + n, ((r - 1) * NC, r * NC))
+            copy(q, "wc", S, src[0], src[2], "lS%d" % (r + 1))
+            copy(q, "wcp", S, src[1], src[2], "lS%d" % (r + 1))
+            if r:
+                q.wait_ge(sem["sS%d" % (r - 1)], 16)
+        else:
+            q.wait_ge(sem["sS%d" % (r - 1)], 16)
+        q.activation(T.yb[:, S[0]:S[1]], T.ps[:, 512 * (6 + r % 2):512 * (6 + r % 2) + NC],
+                     ActivationFunctionType.Copy).then_inc(sem["cS%d" % r], 1)
+        q.wait_ge(sem["cS%d" % r], 1)
+        j = first(singles[r][0], singles[r][1])
+        q.dma_start(T.y[:, j:j + NC], T.yb[:, S[0]:S[1]]).then_inc(sem["sS%d" % r], 16)
+    g.sync.wait_ge(sem.sD3, 16)
+    g.scalar.wait_ge(sem.sS3, 16)

@@ -108,46 +108,60 @@ def plan(L, topo):
             send(c, [(s, cols, [(L["pair"][c], d, dcols)], onchip(c), r)], local)
 
     qx, qg = (0, NC), (NC, 2 * NC)
+
+    def x_out(c):
+        wait(c, "vq")
+        pass_on(c, ("qa", "qap"), qx, ("qa", "qap"), qg, ("rQ", "rR"), "ls")
+
+    via = {}
+    for c in L["inner"][home]:
+        via[c] = []
+        for k in away:
+            m = [v for v in range(SIM) if topo.mates(topo.chip(v), chips[k]) and topo.die(v) == topo.die(c)
+                 and topo.may_write(v, L["port"][k][0])][0]
+            via[c].append(m)
+            for kind in "BT":
+                wait(m, "r%s%d" % (kind, rank(c)))
+                send(m, [piece(kind, rank(c), L["port"][k], topo.mask(m, L["port"][k][0]))])
+
     for k in range(len(chips)):
         ports, inners = L["port"][k], L["inner"][k]
         for c in inners:
-            i = rank(c)
             if k == home:
-                e = L["pair"][c]
-                e2 = [s for s in ports if s != e][0]
-                l2 = [s for s in inners if s != c][0]
-                for kind, other in (("A", e2), ("Z", e2), ("B", l2), ("T", l2)):
-                    wait(c, "i" + kind)
-                    send(c, [piece(kind, i, [e], part(onchip(c), 0, 2)), piece(kind, i, [other], part(onchip(c), 1, 2))])
-            wait(c, "vq")
-            pass_on(c, ("qa", "qap"), qx, ("qa", "qap"), qg, ("rQ", "rR"), "ls")
-            c_out(c)
-            wait(c, "v1", "rDG", "rDH")
-            pass_on(c, ("qb", "qbp"), None, ("qb", "qbp"), None, ("rh", "ri"), "lsG")
-        for c in ports:
-            i = rank(c)
-            if k == home:
-                off = offchip(c)
-                on = onchip(c) & ~off
-                l = rank(L["pair"][c])
-                e2 = [s for s in ports if s != c]
-                wants_a = [s for v in away for s in L["port"][v]]
-                wants_b = [s for v in away for s in L["inner"][v]]
+                i, off = rank(c), offchip(c)
                 for kind in "AZ":
                     wait(c, "i" + kind)
-                    send(c, [piece(kind, i, wants_a, off), piece(kind, i, e2, on)])
-                for kind in "AZ":
-                    wait(c, "r%s%d" % (kind, l))
-                    send(c, [piece(kind, l, wants_a, off)])
+                    send(c, [piece(kind, i, [L["pair"][c]], part(onchip(c), 0, 2)),
+                             piece(kind, i, [s for s in inners if s != c], part(onchip(c), 1, 2))])
                 for kind in "BT":
-                    wait(c, "i" + kind, "r%s%d" % (kind, l))
-                    send(c, [piece(kind, i, wants_b, part(off, 0, 2)), piece(kind, l, wants_b, part(off, 1, 2)),
-                             piece(kind, i, inners, on)])
+                    wait(c, "i" + kind)
+                    send(c, [piece(kind, i, via[c], off), piece(kind, i, ports, onchip(c) & ~off)])
             c_out(c)
             wait(c, "v1")
             pass_on(c, ("qb", "qbp"), None, ("qa", "qap"), qg, ("rG", "rH"), "lsG")
             wait(c, "v2")
             pass_on(c, ("qb", "qbp"), None, ("dG", "dH"), None, ("rDG", "rDH"), "ls")
+        for c in ports:
+            if k == home:
+                i, l, off = rank(c), rank(L["pair"][c]), offchip(c)
+                on = onchip(c) & ~off
+                wants_a = [s for v in away for s in L["inner"][v]]
+                wants_b = [s for v in away for s in L["port"][v]]
+                for kind in "AZ":
+                    wait(c, "i" + kind)
+                    send(c, [piece(kind, i, wants_a, off), piece(kind, i, inners, on)])
+                x_out(c)
+                for kind in "AZ":
+                    wait(c, "r%s%d" % (kind, l))
+                    send(c, [piece(kind, l, wants_a, off)])
+                for kind in "BT":
+                    wait(c, "i" + kind)
+                    send(c, [piece(kind, i, wants_b, off), piece(kind, i, [s for s in ports if s != c], on)])
+            else:
+                x_out(c)
+            c_out(c)
+            wait(c, "v1", "rDG", "rDH")
+            pass_on(c, ("qb", "qbp"), None, ("qb", "qbp"), None, ("rh", "ri"), "lsG")
         for n in range(2):
             c = L["gather"][k][n]
             for buf, kind, r in (("wc", "W", "rC%d"), ("wcp", "V", "rP%d")):
@@ -232,7 +246,7 @@ def rank_program(g, core, T, topo):
         return
     me = L["chips"].index(topo.chip(core))
     mine = L["ranks"][me].index(core)
-    porty = core in L["port"][me]
+    first_layer = core in L["inner"][me]
 
     if me != L["home"]:
         g.sync.dma_start(T.tx[:], T.x[:]).then_inc(sem.ix, 16)
@@ -250,11 +264,10 @@ def rank_program(g, core, T, topo):
     remote()
 
     order = [L["cores"].index(c) for c in L["port"][L["home"]] + L["inner"][L["home"]]]
-    kind = "AZ" if porty else "BT"
+    kind = "AZ" if first_layer else "BT"
 
     def load(q, k, name, after):
         i, s = order[k], ((k % 2) * NC, (k % 2) * NC + NC)
-        h = "i" if i == rank else "r"
         for x in kind:
             wait(q, "i" + x if i == rank else "r%s%d" % (x, i))
         if after:
@@ -288,15 +301,14 @@ def rank_program(g, core, T, topo):
     g.vector.quantize_mx(T.qa[:, 0:NC], T.qap[:, 0:NC], T.tx[:, 0:G * NC]).then_inc(sem.vq, 1)
     load(g.sync, 0, "lW0", None)
     load(g.scalar, 1, "lW1", None)
-    if porty:
+    if first_layer:
         wait(g.tensor, "vq", "rQ", "rR")
         for k in range(G):
             g.tensor.wait_ge(sem["lW%d" % k], 32)
             product(k, "w", k % 2, "qa", (0, 2 * NC), "mP%d" % k)
         load(g.sync, 2, "lW2", "mP0")
-        step(0, 0, "mP%d", "aP%d")
         load(g.scalar, 3, "lW3", "mP1")
-        for k in (1, 2, 3):
+        for k in range(G):
             step(k, 0, "mP%d", "aP%d")
         quantise("aP%d", "v1")
         g.scalar.wait_ge(sem.v1, 1)
@@ -395,9 +407,7 @@ def rank_program(g, core, T, topo):
                 src = ("dW" + n, "dV" + n, ((r - 1) * NC, r * NC))
             copy(q, "wc", S, src[0], src[2], "lS%d" % (r + 1))
             copy(q, "wcp", S, src[1], src[2], "lS%d" % (r + 1))
-            if r:
-                q.wait_ge(sem["sS%d" % (r - 1)], 16)
-        else:
+        if r:
             q.wait_ge(sem["sS%d" % (r - 1)], 16)
         q.activation(T.yb[:, S[0]:S[1]], T.ps[:, 512 * (6 + r % 2):512 * (6 + r % 2) + NC],
                      ActivationFunctionType.Copy).then_inc(sem["cS%d" % r], 1)

@@ -16,10 +16,11 @@ SCRATCH = {
     "yb": ("sbuf", [128, 3 * NC], "float32"),
     "ps": ("psum", [128, 8 * 512], "float32"),
     "dG": ("dram", [128, NC], X4), "dH": ("dram", [128, NC], "uint8"),
+    "dU": ("dram", [128, NC], X4), "dN": ("dram", [128, NC], "uint8"),
     "dX": ("dram", [128, NC], X4), "dY": ("dram", [128, NC], "uint8"),
 }
-SEMAPHORES = ["iA", "iZ", "iB", "iT", "iC", "ix", "ls", "lsC", "lsG", "vq", "v1", "v2", "lG",
-              "rQ", "rR", "rG", "rH", "rDG", "rDH", "rh", "ri"]
+SEMAPHORES = ["iA", "iZ", "iB", "iT", "iC", "iD", "ix", "ls", "lsG", "vq", "v1", "v2", "lG",
+              "rQ", "rR", "rG", "rH", "rDG", "rDH", "rh", "ri", "rE", "rF", "rU", "rN"]
 for _i in range(G):
     for _n, _t, _d in (("dA%d", X4, NC), ("dZ%d", "uint8", NC), ("dB%d", X4, NC), ("dT%d", "uint8", NC)):
         SCRATCH[_n % _i] = ("dram", [128, _d], _t)
@@ -30,7 +31,7 @@ for _c in range(3):
         SCRATCH["dW%d%d" % (_c, _i)] = ("dram", [128, 2 * NC], X4)
         SCRATCH["dV%d%d" % (_c, _i)] = ("dram", [128, 2 * NC], "uint8")
         SEMAPHORES += ["rW%d%d" % (_c, _i), "rV%d%d" % (_c, _i)]
-PLANES = ("wp", "wcp", "qap", "qbp", "dH", "dY")
+PLANES = ("wp", "wcp", "qap", "qbp", "dH", "dY", "dN")
 
 
 def bits(mask):
@@ -90,22 +91,20 @@ def plan(L, topo):
         return (name, None, [(d, name, None) for d in dsts], mask, "r%s%s" % (kind, i))
 
     def c_out(c):
-        m = L["ranks"][where(c)]
-        k, rest = m.index(c), [s for s in m if s != c]
-        col = lambda n: (n * NC, n * NC + NC)
-        keep = (L["gather"][where(c)][k // 2], k % 2)
-        wait(c, "iC")
-        for buf, last, r in (("wc", "dX", "rC%d"), ("wcp", "dY", "rP%d")):
-            if k < 3:
-                ts = [(buf, col(k), [(s, buf, col(k)) for s in rest] + [(keep[0], buf, col(keep[1]))], onchip(c), r % k)]
-            else:
-                ts = [(last, None, [(s, last, None) for s in rest], part(onchip(c), 1, 2), r % k),
-                      (last, None, [(keep[0], buf, col(keep[1]))], part(onchip(c), 0, 2), r % k)]
-            send(c, ts, "lsC")
+        k = L["ranks"][where(c)].index(c)
+        col = ((k % 2) * NC, (k % 2) * NC + NC)
+        for src, buf, i, r in (("dX", "wc", "iC", "rC%d"), ("dY", "wcp", "iD", "rP%d")):
+            wait(c, i)
+            send(c, [(src, None, [(L["gather"][where(c)][k // 2], buf, col)], onchip(c), r % k)])
 
     def pass_on(c, src, cols, dst, dcols, sems, local):
         for s, d, r in zip(src, dst, sems):
             send(c, [(s, cols, [(L["pair"][c], d, dcols)], onchip(c), r)], local)
+
+    def again(c, kinds, tile, dsts):
+        for kind in kinds:
+            wait(c, "r%s%d" % (kind, tile))
+            send(c, [piece(kind, tile, dsts, onchip(c))])
 
     qx, qg = (0, NC), (NC, 2 * NC)
 
@@ -136,7 +135,12 @@ def plan(L, topo):
                 for kind in "BT":
                     wait(c, "i" + kind)
                     send(c, [piece(kind, i, via[c], off), piece(kind, i, ports, onchip(c) & ~off)])
-            c_out(c)
+                c_out(c)
+            else:
+                c_out(c)
+                e = [v for v in L["port"][home] if topo.die(v) == topo.die(c)][0]
+                for t in (e, L["pair"][e]):
+                    again(c, "AZ", rank(t), [s for s in inners if s != c])
             wait(c, "v1")
             pass_on(c, ("qb", "qbp"), None, ("qa", "qap"), qg, ("rG", "rH"), "lsG")
             wait(c, "v2")
@@ -145,8 +149,8 @@ def plan(L, topo):
             if k == home:
                 i, l, off = rank(c), rank(L["pair"][c]), offchip(c)
                 on = onchip(c) & ~off
-                wants_a = [s for v in away for s in L["inner"][v]]
-                wants_b = [s for v in away for s in L["port"][v]]
+                wants_a = [s for v in away for s in L["inner"][v] if topo.die(s) == topo.die(c)]
+                wants_b = [s for v in away for s in L["port"][v] if topo.die(s) == topo.die(c)]
                 for kind in "AZ":
                     wait(c, "i" + kind)
                     send(c, [piece(kind, i, wants_a, off), piece(kind, i, inners, on)])
@@ -157,18 +161,30 @@ def plan(L, topo):
                 for kind in "BT":
                     wait(c, "i" + kind)
                     send(c, [piece(kind, i, wants_b, off), piece(kind, i, [s for s in ports if s != c], on)])
+                c_out(c)
             else:
                 x_out(c)
-            c_out(c)
+                c_out(c)
+                e = [v for v in L["port"][home] if topo.die(v) == topo.die(c)][0]
+                again(c, "BT", rank(e), [s for s in ports if s != c])
             wait(c, "v1", "rDG", "rDH")
             pass_on(c, ("qb", "qbp"), None, ("qb", "qbp"), None, ("rh", "ri"), "lsG")
         for n in range(2):
             c = L["gather"][k][n]
+            both = (0, 2 * NC)
             for buf, kind, r in (("wc", "W", "rC%d"), ("wcp", "V", "rP%d")):
                 name = "%s%d%d" % (kind, k, n)
                 wait(c, r % (2 * n), r % (2 * n + 1))
-                send(c, [(buf, (0, 2 * NC), [(L["scatter"][v][n], "d" + name, None) for v in range(len(chips)) if v != k],
+                send(c, [(buf, both, [(L["scatter"][v][n], "d" + name, None) for v in range(len(chips)) if v != k],
                           offchip(c), "r" + name)])
+            on = onchip(c) & ~offchip(c)
+            for buf, kind, r2, r3 in (("wc", "W", "rE", "rU"), ("wcp", "V", "rF", "rN")):
+                if n == 0:
+                    send(c, [(buf, both, [(s, buf, both) for s in L["ranks"][k]], on, "r%s%d0" % (kind, k))])
+                else:
+                    send(c, [(buf, (0, NC), [(s, buf, (2 * NC, 3 * NC)) for s in L["ranks"][k]], part(on, 0, 2), r2),
+                             (buf, (NC, 2 * NC), [(s, "dU" if kind == "W" else "dN", None) for s in L["ranks"][k]],
+                              part(on, 1, 2), r3)])
             c = L["scatter"][k][n]
             for v in near(L, topo, k):
                 for kind in "WV":
@@ -204,9 +220,8 @@ def rank_program(g, core, T, topo):
     if core not in prog:
         return
     count = totals(prog, core)
-    for s in ("iA", "iZ", "iB", "iT", "ix"):
+    for s in ("iA", "iZ", "iB", "iT", "iC", "iD", "ix"):
         count[s] = 16
-    count["iC"] = 32
     for s in ("vq", "v1", "v2"):
         count[s] = 1
     sem = T.sem
@@ -245,7 +260,6 @@ def rank_program(g, core, T, topo):
         remote()
         return
     me = L["chips"].index(topo.chip(core))
-    mine = L["ranks"][me].index(core)
     first_layer = core in L["inner"][me]
 
     if me != L["home"]:
@@ -256,14 +270,13 @@ def rank_program(g, core, T, topo):
         g.sync.dma_start(T.tx[:], T.x[:]).then_inc(sem.ix, 16)
         g.scalar.dma_start(view("dB%d" % rank, None), T.bc[:]).then_inc(sem.iB, 16)
         g.sync.dma_start(view("dT%d" % rank, None), T.bs[:]).then_inc(sem.iT, 16)
-    slot = (mine * NC, mine * NC + NC)
-    own = (("wc", slot), ("wcp", slot)) if mine < 3 else (("dX", None), ("dY", None))
-    g.scalar.dma_start(view(own[0][0], own[0][1]), T.cc[:]).then_inc(sem.iC, 16)
-    g.sync.dma_start(view(own[1][0], own[1][1]), T.cs[:]).then_inc(sem.iC, 16)
+    g.scalar.dma_start(view("dX", None), T.cc[:]).then_inc(sem.iC, 16)
+    g.sync.dma_start(view("dY", None), T.cs[:]).then_inc(sem.iD, 16)
 
     remote()
 
-    order = [L["cores"].index(c) for c in L["port"][L["home"]] + L["inner"][L["home"]]]
+    own = lambda c: 0 if topo.die(c) == topo.die(core) else 1
+    order = [L["cores"].index(c) for kind in ("port", "inner") for c in sorted(L[kind][L["home"]], key=own)]
     kind = "AZ" if first_layer else "BT"
 
     def load(q, k, name, after):
@@ -353,14 +366,15 @@ def rank_program(g, core, T, topo):
     first = lambda ch, i: L["cores"].index(L["ranks"][ch][i]) * NC
     D, S = (0, 2 * NC), (2 * NC, 3 * NC)
 
-    def arrived(q, k, kinds):
-        if k == mine:
-            wait(q, "iC")
-        else:
-            wait(q, *[x % k for x in kinds])
+    def load_single(r):
+        n = "%d1" % b
+        names = ("dU", "dN", "rU", "rN") if r == 1 else ("dW" + n, "dV" + n, "rW" + n, "rV" + n)
+        cols = None if r == 1 else ((r % 2) * NC, (r % 2) * NC + NC)
+        wait(g.scalar, names[2], names[3])
+        copy(g.scalar, "wc", S, names[0], cols, "lS%d" % r)
+        copy(g.scalar, "wcp", S, names[1], cols, "lS%d" % r)
 
-    for k in range(3):
-        arrived(g.tensor, k, ("rC%d", "rP%d"))
+    wait(g.tensor, "rW%d0" % me, "rV%d0" % me, "rE", "rF")
     for r in range(4):
         if r:
             g.tensor.wait_ge(sem["lS%d" % r], 32)
@@ -375,8 +389,6 @@ def rank_program(g, core, T, topo):
         product(5, "wc", 1, "qb", (0, NC), "mE%d" % r)
 
     for r in range(4):
-        if r == 0:
-            wait(g.sync, "lsC")
         if r < 3:
             n = "%d%d" % pairs[r + 1]
             wait(g.sync, "rW" + n, "rV" + n)
@@ -384,29 +396,22 @@ def rank_program(g, core, T, topo):
             g.sync.wait_ge(sem["mE%d" % r], 1)
             copy(g.sync, "wc", D, "dW" + n, None, "lD%d" % (r + 1))
             copy(g.sync, "wcp", D, "dV" + n, None, "lD%d" % (r + 1))
+        j = first(pairs[r][0], 2 * pairs[r][1])
         for n, m, c in ((0, "mD%d", "cD%d"), (1, "mE%d", "cE%d")):
             g.vector.wait_ge(sem[m % r], 1)
             if r:
                 g.vector.wait_ge(sem["sD%d" % (r - 1)], 16)
             g.vector.tensor_copy(T.yb[:, n * NC:n * NC + NC], T.ps[:, 512 * (4 + n):512 * (4 + n) + NC]).then_inc(sem[c % r], 1)
             g.sync.wait_ge(sem[c % r], 1)
-        j = first(pairs[r][0], 2 * pairs[r][1])
-        g.sync.dma_start(T.y[:, j:j + 2 * NC], T.yb[:, D[0]:D[1]]).then_inc(sem["sD%d" % r], 16)
+            if r == 3:
+                g.sync.dma_start(T.y[:, j + n * NC:j + n * NC + NC], T.yb[:, n * NC:n * NC + NC]).then_inc(sem.sD3, 16)
+        if r < 3:
+            g.sync.dma_start(T.y[:, j:j + 2 * NC], T.yb[:, D[0]:D[1]]).then_inc(sem["sD%d" % r], 16)
     for r in range(4):
         q = g.scalar
-        if r == 0:
-            wait(q, "lsC")
         q.wait_ge(sem["mS%d" % r], 1)
         if r < 3:
-            if r == 0:
-                arrived(q, 3, ("rC%d", "rP%d"))
-                src = ("dX", "dY", None)
-            else:
-                n = "%d1" % b
-                wait(q, "rW" + n, "rV" + n)
-                src = ("dW" + n, "dV" + n, ((r - 1) * NC, r * NC))
-            copy(q, "wc", S, src[0], src[2], "lS%d" % (r + 1))
-            copy(q, "wcp", S, src[1], src[2], "lS%d" % (r + 1))
+            load_single(r + 1)
         if r:
             q.wait_ge(sem["sS%d" % (r - 1)], 16)
         q.activation(T.yb[:, S[0]:S[1]], T.ps[:, 512 * (6 + r % 2):512 * (6 + r % 2) + NC],
@@ -414,5 +419,5 @@ def rank_program(g, core, T, topo):
         q.wait_ge(sem["cS%d" % r], 1)
         j = first(singles[r][0], singles[r][1])
         q.dma_start(T.y[:, j:j + NC], T.yb[:, S[0]:S[1]]).then_inc(sem["sS%d" % r], 16)
-    g.sync.wait_ge(sem.sD3, 16)
+    g.sync.wait_ge(sem.sD3, 32)
     g.scalar.wait_ge(sem.sS3, 16)

@@ -9,39 +9,39 @@ X4 = "float8_e4m3fn_x4"
 SCRATCH = {
     "tx": ("sbuf", [128, G * NC], "bfloat16"),
     "tg": ("sbuf", [128, G * NC], "bfloat16"),
-    "qa": ("sbuf", [128, 2 * NC], X4), "qap": ("sbuf", [128, 2 * NC], "uint8"),
-    "qb": ("sbuf", [128, NC], X4), "qbp": ("sbuf", [128, NC], "uint8"),
+    "q": ("sbuf", [128, 3 * NC], X4), "qp": ("sbuf", [128, 3 * NC], "uint8"),
     "w": ("sbuf", [128, 2 * NC], X4), "wp": ("sbuf", [128, 2 * NC], "uint8"),
     "wc": ("sbuf", [128, 3 * NC], X4), "wcp": ("sbuf", [128, 3 * NC], "uint8"),
     "yb": ("sbuf", [128, 3 * NC], "float32"),
     "ps": ("psum", [128, 8 * 512], "float32"),
-    "dG": ("dram", [128, NC], X4), "dH": ("dram", [128, NC], "uint8"),
-    "dU": ("dram", [128, NC], X4), "dN": ("dram", [128, NC], "uint8"),
     "dX": ("dram", [128, NC], X4), "dY": ("dram", [128, NC], "uint8"),
 }
-SEMAPHORES = ["iA", "iZ", "iB", "iT", "iC", "iD", "ix", "ls", "lsG", "vq", "v1", "v2", "lG",
-              "rQ", "rR", "rG", "rH", "rDG", "rDH", "rh", "ri", "rE", "rF", "rU", "rN"]
+SEMAPHORES = ["iA", "iZ", "iB", "iT", "iC", "iD", "ix", "ls", "lsG", "vq", "v1", "v2",
+              "rQ", "rR", "rG", "rH", "rDG", "rDH", "rh", "ri"]
 for _i in range(G):
-    for _n, _t, _d in (("dA%d", X4, NC), ("dZ%d", "uint8", NC), ("dB%d", X4, NC), ("dT%d", "uint8", NC)):
-        SCRATCH[_n % _i] = ("dram", [128, _d], _t)
-    SEMAPHORES += [s % _i for s in ("rA%d", "rZ%d", "rB%d", "rT%d", "rC%d", "rP%d", "lW%d", "lV%d", "mP%d", "mQ%d", "aP%d", "aQ%d",
-                                    "mD%d", "mE%d", "mS%d", "cD%d", "cE%d", "cS%d", "lD%d", "lS%d", "sD%d", "sS%d")]
+    for _n, _t in (("dA%d", X4), ("dZ%d", "uint8"), ("dB%d", X4), ("dT%d", "uint8"), ("dC%d", X4), ("dP%d", "uint8")):
+        SCRATCH[_n % _i] = ("dram", [128, NC], _t)
+    SEMAPHORES += [s % _i for s in ("rA%d", "rZ%d", "rB%d", "rT%d", "rC%d", "rP%d", "lW%d", "mP%d", "aP%d", "aQ%d")]
+SEMAPHORES += ["lV0", "lV1", "mQ0", "mQ1"]
+for _r in range(4):
+    SEMAPHORES += [s % (_r, _i) for _i in range(3) for s in ("mC%d%d", "cC%d%d")]
+    SEMAPHORES += [s % (_n, _r) for _n in range(2) for s in ("lC%d%d", "sC%d%d")]
 for _c in range(3):
     for _i in range(2):
         SCRATCH["dW%d%d" % (_c, _i)] = ("dram", [128, 2 * NC], X4)
         SCRATCH["dV%d%d" % (_c, _i)] = ("dram", [128, 2 * NC], "uint8")
         SEMAPHORES += ["rW%d%d" % (_c, _i), "rV%d%d" % (_c, _i)]
-PLANES = ("wp", "wcp", "qap", "qbp", "dH", "dY", "dN")
+PLANES = ("wp", "wcp", "qp", "dY")
+LEFT, RIGHT, THIRD = (0, NC), (NC, 2 * NC), (2 * NC, 3 * NC)
 
 
 def bits(mask):
     return [b for b in range(16) if mask >> b & 1]
 
 
-def part(mask, k, n):
+def half(mask):
     b = bits(mask)
-    m = len(b) // n
-    return sum(1 << e for e in b[k * m:k * m + m])
+    return sum(1 << e for e in b[:len(b) // 2])
 
 
 def layout(T, topo):
@@ -91,26 +91,21 @@ def plan(L, topo):
         return (name, None, [(d, name, None) for d in dsts], mask, "r%s%s" % (kind, i))
 
     def c_out(c):
-        k = L["ranks"][where(c)].index(c)
+        ranks = L["ranks"][where(c)]
+        k = ranks.index(c)
         col = ((k % 2) * NC, (k % 2) * NC + NC)
-        for src, buf, i, r in (("dX", "wc", "iC", "rC%d"), ("dY", "wcp", "iD", "rP%d")):
+        for src, buf, i, kind in (("dX", "wc", "iC", "C%d" % k), ("dY", "wcp", "iD", "P%d" % k)):
             wait(c, i)
-            send(c, [(src, None, [(L["gather"][where(c)][k // 2], buf, col)], onchip(c), r % k)])
+            send(c, [(src, None, [(L["gather"][where(c)][k // 2], buf, col)] + [(s, "d" + kind, None) for s in ranks if s != c],
+                      onchip(c), "r" + kind)])
 
-    def pass_on(c, src, cols, dst, dcols, sems, local):
-        for s, d, r in zip(src, dst, sems):
-            send(c, [(s, cols, [(L["pair"][c], d, dcols)], onchip(c), r)], local)
-
-    def again(c, kinds, tile, dsts):
-        for kind in kinds:
-            wait(c, "r%s%d" % (kind, tile))
-            send(c, [piece(kind, tile, dsts, onchip(c))])
-
-    qx, qg = (0, NC), (NC, 2 * NC)
+    def pass_on(c, cols, dcols, sems, local="ls"):
+        for q, r in zip(("q", "qp"), sems):
+            send(c, [(q, cols, [(L["pair"][c], q, dcols)], onchip(c), r)], local)
 
     def x_out(c):
         wait(c, "vq")
-        pass_on(c, ("qa", "qap"), qx, ("qa", "qap"), qg, ("rQ", "rR"), "ls")
+        pass_on(c, LEFT, RIGHT, ("rQ", "rR"))
 
     via = {}
     for c in L["inner"][home]:
@@ -126,12 +121,14 @@ def plan(L, topo):
     for k in range(len(chips)):
         ports, inners = L["port"][k], L["inner"][k]
         for c in inners:
+            other = [s for s in inners if s != c]
             if k == home:
-                i, off = rank(c), offchip(c)
+                i, off, part = rank(c), offchip(c), half(onchip(c))
                 for kind in "AZ":
                     wait(c, "i" + kind)
-                    send(c, [piece(kind, i, [L["pair"][c]], part(onchip(c), 0, 2)),
-                             piece(kind, i, [s for s in inners if s != c], part(onchip(c), 1, 2))])
+                    send(c, [piece(kind, i, [L["pair"][c]], part)])
+                for kind in "AZ":
+                    send(c, [piece(kind, i, other, part)])
                 for kind in "BT":
                     wait(c, "i" + kind)
                     send(c, [piece(kind, i, via[c], off), piece(kind, i, ports, onchip(c) & ~off)])
@@ -139,52 +136,51 @@ def plan(L, topo):
             else:
                 c_out(c)
                 e = [v for v in L["port"][home] if topo.die(v) == topo.die(c)][0]
-                for t in (e, L["pair"][e]):
-                    again(c, "AZ", rank(t), [s for s in inners if s != c])
+                for kind, buf in (("A", "w"), ("Z", "wp")):
+                    name = "%s%d" % (kind, rank(e))
+                    wait(c, "r" + name)
+                    send(c, [("d" + name, None, [(s, buf, RIGHT) for s in other], onchip(c), "r" + name)])
+                for kind in "AZ":
+                    wait(c, "r%s%d" % (kind, rank(L["pair"][e])))
+                    send(c, [piece(kind, rank(L["pair"][e]), other, onchip(c))])
             wait(c, "v1")
-            pass_on(c, ("qb", "qbp"), None, ("qa", "qap"), qg, ("rG", "rH"), "lsG")
+            pass_on(c, THIRD, RIGHT, ("rG", "rH"), "lsG")
             wait(c, "v2")
-            pass_on(c, ("qb", "qbp"), None, ("dG", "dH"), None, ("rDG", "rDH"), "ls")
+            pass_on(c, THIRD, THIRD, ("rDG", "rDH"))
         for c in ports:
             if k == home:
                 i, l, off = rank(c), rank(L["pair"][c]), offchip(c)
                 on = onchip(c) & ~off
-                wants_a = [s for v in away for s in L["inner"][v] if topo.die(s) == topo.die(c)]
-                wants_b = [s for v in away for s in L["port"][v] if topo.die(s) == topo.die(c)]
+                same = lambda group: [s for v in away for s in L[group][v] if topo.die(s) == topo.die(c)]
                 for kind in "AZ":
                     wait(c, "i" + kind)
-                    send(c, [piece(kind, i, wants_a, off), piece(kind, i, inners, on)])
+                    send(c, [piece(kind, i, same("inner"), off)])
+                for kind in "AZ":
+                    send(c, [piece(kind, i, inners, on)])
                 x_out(c)
                 for kind in "AZ":
                     wait(c, "r%s%d" % (kind, l))
-                    send(c, [piece(kind, l, wants_a, off)])
+                    send(c, [piece(kind, l, same("inner"), off)])
                 for kind in "BT":
                     wait(c, "i" + kind)
-                    send(c, [piece(kind, i, wants_b, off), piece(kind, i, [s for s in ports if s != c], on)])
+                    send(c, [piece(kind, i, same("port"), off), piece(kind, i, [s for s in ports if s != c], on)])
                 c_out(c)
             else:
                 x_out(c)
                 c_out(c)
                 e = [v for v in L["port"][home] if topo.die(v) == topo.die(c)][0]
-                again(c, "BT", rank(e), [s for s in ports if s != c])
+                for kind in "BT":
+                    wait(c, "r%s%d" % (kind, rank(e)))
+                    send(c, [piece(kind, rank(e), [s for s in ports if s != c], onchip(c))])
             wait(c, "v1", "rDG", "rDH")
-            pass_on(c, ("qb", "qbp"), None, ("qb", "qbp"), None, ("rh", "ri"), "lsG")
+            pass_on(c, RIGHT, THIRD, ("rh", "ri"))
         for n in range(2):
             c = L["gather"][k][n]
-            both = (0, 2 * NC)
             for buf, kind, r in (("wc", "W", "rC%d"), ("wcp", "V", "rP%d")):
                 name = "%s%d%d" % (kind, k, n)
                 wait(c, r % (2 * n), r % (2 * n + 1))
-                send(c, [(buf, both, [(L["scatter"][v][n], "d" + name, None) for v in range(len(chips)) if v != k],
+                send(c, [(buf, (0, 2 * NC), [(L["scatter"][v][n], "d" + name, None) for v in range(len(chips)) if v != k],
                           offchip(c), "r" + name)])
-            on = onchip(c) & ~offchip(c)
-            for buf, kind, r2, r3 in (("wc", "W", "rE", "rU"), ("wcp", "V", "rF", "rN")):
-                if n == 0:
-                    send(c, [(buf, both, [(s, buf, both) for s in L["ranks"][k]], on, "r%s%d0" % (kind, k))])
-                else:
-                    send(c, [(buf, (0, NC), [(s, buf, (2 * NC, 3 * NC)) for s in L["ranks"][k]], part(on, 0, 2), r2),
-                             (buf, (NC, 2 * NC), [(s, "dU" if kind == "W" else "dN", None) for s in L["ranks"][k]],
-                              part(on, 1, 2), r3)])
             c = L["scatter"][k][n]
             for v in near(L, topo, k):
                 for kind in "WV":
@@ -233,10 +229,7 @@ def rank_program(g, core, T, topo):
     def view(name, cols):
         t = T[name]
         v = t[:, 0:t.shape[1]] if cols is None else t[:, cols[0]:cols[1]]
-        return v if name in PLANES or name[:2] in ("dZ", "dT", "dV") else v.bitcast(dt.uint8)
-
-    def copy(q, dst, dcols, src, scols, name):
-        q.dma_start(view(dst, dcols), view(src, scols)).then_inc(sem[name], 16)
+        return v if name in PLANES or name[:2] in ("dZ", "dT", "dV", "dP") else v.bitcast(dt.uint8)
 
     def remote():
         for op in prog[core]:
@@ -252,8 +245,7 @@ def rank_program(g, core, T, topo):
                 ts.append(RemoteDMATransfer(dst_ids=ids, dma_engine_mask=mask, remote_sem=sem[rsem], srcs=[view(src, cols)],
                                             dsts=[view(d[1], d[2]) for d in dsts]))
             g.remote_dma_fused(ts, local_sem=sem[op[2]])
-        if "ls" in count:
-            wait(g, "ls")
+        wait(g, "ls")
 
     rank = T.rank_of(core)
     if rank is None:
@@ -277,147 +269,142 @@ def rank_program(g, core, T, topo):
 
     own = lambda c: 0 if topo.die(c) == topo.die(core) else 1
     order = [L["cores"].index(c) for kind in ("port", "inner") for c in sorted(L[kind][L["home"]], key=own)]
+    order.sort(key=lambda i: i != rank)
     kind = "AZ" if first_layer else "BT"
+    own_in = {"A": T.ac, "Z": T.az, "B": T.bc, "T": T.bs}
+    landed = first_layer and me != L["home"]
 
     def load(q, k, name, after):
-        i, s = order[k], ((k % 2) * NC, (k % 2) * NC + NC)
-        for x in kind:
-            wait(q, "i" + x if i == rank else "r%s%d" % (x, i))
+        i, s = order[k], RIGHT if k % 2 else LEFT
+        if i != rank:
+            wait(q, *["r%s%d" % (x, i) for x in kind])
         if after:
             q.wait_ge(sem[after], 1)
-        copy(q, "w", s, "d%s%d" % (kind[0], i), None, name)
-        copy(q, "wp", s, "d%s%d" % (kind[1], i), None, name)
+        for x, buf in zip(kind, ("w", "wp")):
+            src = own_in[x][:] if i == rank else view("d%s%d" % (x, i), None)
+            q.dma_start(view(buf, s), src).then_inc(sem[name], 16)
 
-    def product(bank, w, s, q, cols, done):
+    def product(bank, w, s, cols, done):
         n = cols[1] - cols[0]
         g.tensor.matmul_mx(T.ps[:, 512 * bank:512 * bank + n], T[w][:, s * NC:s * NC + NC], T[w + "p"][:, s * NC:s * NC + NC],
-                           T[q][:, cols[0]:cols[1]], T[q + "p"][:, cols[0]:cols[1]], True, True).then_inc(sem[done], 1)
+                           T.q[:, cols[0]:cols[1]], T.qp[:, cols[0]:cols[1]], True, True).then_inc(sem[done], 1)
 
-    def step(k, col, m, a):
-        q = g.vector if k % 2 else g.scalar
-        q.wait_ge(sem[m % k], 1)
-        out, z = T.tg[:, order[k]:G * NC:G], T.ps[:, 512 * k + col:512 * k + col + NC]
-        if k % 2:
-            r = q.tensor_scalar(out, z, SCALE, 0.0, AluOpType.mult, AluOpType.max)
-        else:
-            r = q.activation(out, z, ActivationFunctionType.Relu, scale=SCALE)
-        r.then_inc(sem[a % k], 1)
-
-    def quantise(a, done):
+    def result(jobs, e, cols, done):
+        for k, col, m in jobs:
+            q = g.vector if k % 2 else g.scalar
+            q.wait_ge(sem[m % k], 1)
+            out, z = T.tg[:, order[k]:G * NC:G], T.ps[:, 512 * k + col:512 * k + col + NC]
+            if k % 2:
+                r = q.tensor_scalar(out, z, SCALE, 0.0, AluOpType.mult, AluOpType.max)
+            else:
+                r = q.activation(out, z, ActivationFunctionType.Relu, scale=SCALE)
+            r.then_inc(sem[e % k], 1)
         for k in range(G):
-            g.vector.wait_ge(sem[a % k], 1)
-        if done == "v2":
+            g.vector.wait_ge(sem[e % k], 1)
+        if done == "v2" and first_layer:
             wait(g.vector, "lsG")
-        g.vector.quantize_mx(T.qb[:, 0:NC], T.qbp[:, 0:NC], T.tg[:, 0:G * NC]).then_inc(sem[done], 1)
+        g.vector.quantize_mx(T.q[:, cols[0]:cols[1]], T.qp[:, cols[0]:cols[1]], T.tg[:, 0:G * NC]).then_inc(sem[done], 1)
+        if done == "v1":
+            g.scalar.wait_ge(sem.v1, 1)
+            g.vector.wait_ge(sem.v1, 1)
+
+    ranks = L["ranks"]
+    a, b = near(L, topo, me)
+    lanes = [[(me, 0, 2), (a, 0, 2), (a, 2, 2), (b, 0, 2)], [(me, 2, 1), (me, 3, 1), (b, 2, 1), (b, 3, 1)]]
+    span = [(0, 2 * NC), (2 * NC, 3 * NC)]
+
+    def load_c(q, n, r):
+        v, i, m = lanes[n][r]
+        if v != me:
+            name, cols = "%d%d" % (v, i // 2), ((i % 2) * NC, (i % 2 + m) * NC)
+            wait(q, "rW" + name, "rV" + name)
+            jobs = [(span[n], view("dW" + name, cols), view("dV" + name, cols))]
+        else:
+            jobs = []
+            for h in range(m):
+                s, k = (span[n][0] + h * NC, span[n][0] + h * NC + NC), i + h
+                if ranks[me][k] == core:
+                    jobs.append((s, T.cc[:], T.cs[:]))
+                else:
+                    wait(q, "rC%d" % k, "rP%d" % k)
+                    jobs.append((s, view("dC%d" % k, None), view("dP%d" % k, None)))
+        for s, codes, plane in jobs:
+            q.dma_start(view("wc", s), codes).then_inc(sem["lC%d%d" % (n, r)], 16)
+            q.dma_start(view("wcp", s), plane).then_inc(sem["lC%d%d" % (n, r)], 16)
 
     g.vector.wait_ge(sem.ix, 16)
-    g.vector.quantize_mx(T.qa[:, 0:NC], T.qap[:, 0:NC], T.tx[:, 0:G * NC]).then_inc(sem.vq, 1)
+    g.vector.quantize_mx(T.q[:, 0:NC], T.qp[:, 0:NC], T.tx[:, 0:G * NC]).then_inc(sem.vq, 1)
     load(g.sync, 0, "lW0", None)
-    load(g.scalar, 1, "lW1", None)
+    if not landed:
+        load(g.scalar, 1, "lW1", None)
     if first_layer:
         wait(g.tensor, "vq", "rQ", "rR")
-        for k in range(G):
+    else:
+        for n in range(2):
+            load_c(g.sync, n, 0)
+        wait(g.tensor, "rG", "rH")
+    for k in range(G):
+        if k == 1 and landed:
+            wait(g.tensor, "rA%d" % order[1], "rZ%d" % order[1])
+        else:
             g.tensor.wait_ge(sem["lW%d" % k], 32)
-            product(k, "w", k % 2, "qa", (0, 2 * NC), "mP%d" % k)
-        load(g.sync, 2, "lW2", "mP0")
-        load(g.scalar, 3, "lW3", "mP1")
-        for k in range(G):
-            step(k, 0, "mP%d", "aP%d")
-        quantise("aP%d", "v1")
-        g.scalar.wait_ge(sem.v1, 1)
-        g.vector.wait_ge(sem.v1, 1)
-        for k in range(G):
-            step(k, NC, "mP%d", "aQ%d")
-        quantise("aQ%d", "v2")
+        if first_layer:
+            cols = LEFT[0], RIGHT[1]
+        elif k < 2:
+            cols = RIGHT
+        else:
+            cols = RIGHT[0], THIRD[1]
+            wait(g.tensor, "rDG", "rDH")
+        product(k, "w", k % 2, cols, "mP%d" % k)
+    load(g.sync, 2, "lW2", "mP0")
+    load(g.scalar, 3, "lW3", "mP1")
+    if first_layer:
+        result([(k, 0, "mP%d") for k in range(G)], "aP%d", THIRD, "v1")
+        result([(k, NC, "mP%d") for k in range(G)], "aQ%d", THIRD, "v2")
+        wait(g.sync, "ls")
+        for n in range(2):
+            load_c(g.sync, n, 0)
         wait(g.tensor, "rh", "ri")
     else:
-        wait(g.tensor, "rG", "rH")
-        for k in range(G):
-            g.tensor.wait_ge(sem["lW%d" % k], 32)
-            product(k, "w", k % 2, "qa", (NC, 2 * NC), "mP%d" % k)
-        load(g.sync, 2, "lW2", "mP0")
-        load(g.scalar, 3, "lW3", "mP1")
-        for k in range(G):
-            step(k, 0, "mP%d", "aP%d")
-        quantise("aP%d", "v1")
-        wait(g.sync, "rDG", "rDH")
-        for k in range(G):
-            g.sync.wait_ge(sem["mP%d" % k], 1)
-        copy(g.sync, "qa", (NC, 2 * NC), "dG", None, "lG")
-        copy(g.sync, "qap", (NC, 2 * NC), "dH", None, "lG")
-        g.tensor.wait_ge(sem.lG, 32)
-        for k in (2, 3, 0, 1):
-            if k < 2:
-                g.tensor.wait_ge(sem["lV%d" % k], 32)
+        for k in range(2):
+            load(g.sync, k, "lV%d" % k, "mP%d" % (k + 2))
+            g.tensor.wait_ge(sem["lV%d" % k], 32)
             g.tensor.wait_ge(sem["aP%d" % k], 1)
-            product(k, "w", k % 2, "qa", (NC, 2 * NC), "mQ%d" % k)
-        load(g.sync, 0, "lV0", "mQ2")
-        load(g.scalar, 1, "lV1", "mQ3")
-        g.scalar.wait_ge(sem.v1, 1)
-        g.vector.wait_ge(sem.v1, 1)
-        for k in (2, 3, 0, 1):
-            step(k, 0, "mQ%d", "aQ%d")
-        quantise("aQ%d", "v2")
+            product(k, "w", k, THIRD, "mQ%d" % k)
+        result([(k, 0, "mP%d") for k in range(G)], "aP%d", RIGHT, "v1")
+        result([(2, NC, "mP%d"), (3, NC, "mP%d"), (0, 0, "mQ%d"), (1, 0, "mQ%d")], "aQ%d", THIRD, "v2")
         g.tensor.wait_ge(sem.v2, 1)
 
-    a, b = near(L, topo, me)
-    pairs = [(me, 0), (a, 0), (a, 1), (b, 0)]
-    singles = [(me, 2), (me, 3), (b, 2), (b, 3)]
-    first = lambda ch, i: L["cores"].index(L["ranks"][ch][i]) * NC
-    D, S = (0, 2 * NC), (2 * NC, 3 * NC)
-
-    def load_single(r):
-        n = "%d1" % b
-        names = ("dU", "dN", "rU", "rN") if r == 1 else ("dW" + n, "dV" + n, "rW" + n, "rV" + n)
-        cols = None if r == 1 else ((r % 2) * NC, (r % 2) * NC + NC)
-        wait(g.scalar, names[2], names[3])
-        copy(g.scalar, "wc", S, names[0], cols, "lS%d" % r)
-        copy(g.scalar, "wcp", S, names[1], cols, "lS%d" % r)
-
-    wait(g.tensor, "rW%d0" % me, "rV%d0" % me, "rE", "rF")
+    bank = lambda n, r, h: 6 + r % 2 if n else 4 + h
     for r in range(4):
-        if r:
-            g.tensor.wait_ge(sem["lS%d" % r], 32)
-        if r >= 2:
-            g.tensor.wait_ge(sem["cS%d" % (r - 2)], 1)
-        product(6 + r % 2, "wc", 2, "qb", (0, NC), "mS%d" % r)
-        if r:
-            g.tensor.wait_ge(sem["lD%d" % r], 32)
-            g.tensor.wait_ge(sem["cD%d" % (r - 1)], 1)
-            g.tensor.wait_ge(sem["cE%d" % (r - 1)], 1)
-        product(4, "wc", 0, "qb", (0, NC), "mD%d" % r)
-        product(5, "wc", 1, "qb", (0, NC), "mE%d" % r)
-
-    for r in range(4):
-        if r < 3:
-            n = "%d%d" % pairs[r + 1]
-            wait(g.sync, "rW" + n, "rV" + n)
-            g.sync.wait_ge(sem["mD%d" % r], 1)
-            g.sync.wait_ge(sem["mE%d" % r], 1)
-            copy(g.sync, "wc", D, "dW" + n, None, "lD%d" % (r + 1))
-            copy(g.sync, "wcp", D, "dV" + n, None, "lD%d" % (r + 1))
-        j = first(pairs[r][0], 2 * pairs[r][1])
-        for n, m, c in ((0, "mD%d", "cD%d"), (1, "mE%d", "cE%d")):
-            g.vector.wait_ge(sem[m % r], 1)
-            if r:
-                g.vector.wait_ge(sem["sD%d" % (r - 1)], 16)
-            g.vector.tensor_copy(T.yb[:, n * NC:n * NC + NC], T.ps[:, 512 * (4 + n):512 * (4 + n) + NC]).then_inc(sem[c % r], 1)
-            g.sync.wait_ge(sem[c % r], 1)
-            if r == 3:
-                g.sync.dma_start(T.y[:, j + n * NC:j + n * NC + NC], T.yb[:, n * NC:n * NC + NC]).then_inc(sem.sD3, 16)
-        if r < 3:
-            g.sync.dma_start(T.y[:, j:j + 2 * NC], T.yb[:, D[0]:D[1]]).then_inc(sem["sD%d" % r], 16)
-    for r in range(4):
-        q = g.scalar
-        q.wait_ge(sem["mS%d" % r], 1)
-        if r < 3:
-            load_single(r + 1)
-        if r:
-            q.wait_ge(sem["sS%d" % (r - 1)], 16)
-        q.activation(T.yb[:, S[0]:S[1]], T.ps[:, 512 * (6 + r % 2):512 * (6 + r % 2) + NC],
-                     ActivationFunctionType.Copy).then_inc(sem["cS%d" % r], 1)
-        q.wait_ge(sem["cS%d" % r], 1)
-        j = first(singles[r][0], singles[r][1])
-        q.dma_start(T.y[:, j:j + NC], T.yb[:, S[0]:S[1]]).then_inc(sem["sS%d" % r], 16)
-    g.sync.wait_ge(sem.sD3, 32)
-    g.scalar.wait_ge(sem.sS3, 16)
+        for n in (1, 0):
+            v, i, m = lanes[n][r]
+            g.tensor.wait_ge(sem["lC%d%d" % (n, r)], 32 * (m if v == me else 1))
+            for h in range(m):
+                if r > n:
+                    g.tensor.wait_ge(sem["cC%d%d" % (r - 1 - n, 2 * n + h)], 1)
+                product(bank(n, r, h), "wc", 2 * n + h, THIRD, "mC%d%d" % (r, 2 * n + h))
+    for n, q, cq in ((0, g.sync, g.vector), (1, g.scalar, g.scalar)):
+        for r in range(4):
+            v, i, m = lanes[n][r]
+            for h in range(m):
+                q.wait_ge(sem["mC%d%d" % (r, 2 * n + h)], 1)
+            if r < 3:
+                load_c(q, n, r + 1)
+            j = L["cores"].index(ranks[v][i]) * NC
+            for h in range(m):
+                c = "cC%d%d" % (r, 2 * n + h)
+                y, z = T.yb[:, (2 * n + h) * NC:(2 * n + h) * NC + NC], T.ps[:, 512 * bank(n, r, h):512 * bank(n, r, h) + NC]
+                cq.wait_ge(sem["mC%d%d" % (r, 2 * n + h)], 1)
+                if r and not h:
+                    cq.wait_ge(sem["sC%d%d" % (n, r - 1)], 16)
+                if n:
+                    cq.activation(y, z, ActivationFunctionType.Copy).then_inc(sem[c], 1)
+                else:
+                    cq.tensor_copy(y, z).then_inc(sem[c], 1)
+                q.wait_ge(sem[c], 1)
+                if r == 3:
+                    q.dma_start(T.y[:, j + h * NC:j + h * NC + NC], y).then_inc(sem["sC%d3" % n], 16)
+            if r < 3:
+                q.dma_start(T.y[:, j:j + m * NC], T.yb[:, span[n][0]:span[n][1]]).then_inc(sem["sC%d%d" % (n, r)], 16)
+        q.wait_ge(sem["sC%d3" % n], 16 * lanes[n][3][2])

import numpy
from concourse.bass import DstId, RemoteDMATransfer
from concourse.mybir import dt, AluOpType, ActivationFunctionType

NC, G, NR, SIM = 128, 4, 12, 80
SCALE = float(numpy.float32(0.029))
X4 = "float8_e4m3fn_x4"

SCRATCH = {
    "tx": ("sbuf", [128, G * NC], "bfloat16"),
    "tg": ("sbuf", [128, G * NC], "bfloat16"),
    "q": ("sbuf", [128, 3 * NC], X4), "qp": ("sbuf", [128, 3 * NC], "uint8"),
    "w": ("sbuf", [128, 2 * NC], X4), "wp": ("sbuf", [128, 2 * NC], "uint8"),
    "wc": ("sbuf", [128, 3 * NC], X4), "wcp": ("sbuf", [128, 3 * NC], "uint8"),
    "yb": ("sbuf", [128, 3 * NC], "float32"),
    "ps": ("psum", [128, 8 * 512], "float32"),
    "dX": ("dram", [128, NC], X4), "dY": ("dram", [128, NC], "uint8"),
}
SEMAPHORES = ["iA", "iZ", "iB", "iT", "iC", "iD", "ix", "ls", "lsG", "vq", "v1", "v2",
              "rQ", "rR", "rG", "rH", "rDG", "rDH", "rh", "ri"]
for _i in range(G):
    for _n, _t in (("dA%d", X4), ("dZ%d", "uint8"), ("dB%d", X4), ("dT%d", "uint8"), ("dC%d", X4), ("dP%d", "uint8")):
        SCRATCH[_n % _i] = ("dram", [128, NC], _t)
    SEMAPHORES += [s % _i for s in ("rA%d", "rZ%d", "rB%d", "rT%d", "rC%d", "rP%d", "lW%d", "mP%d", "aP%d", "aQ%d")]
SEMAPHORES += ["lV0", "lV1", "mQ0", "mQ1"]
for _r in range(4):
    SEMAPHORES += [s % (_r, _i) for _i in range(3) for s in ("mC%d%d", "cC%d%d")]
    SEMAPHORES += [s % (_n, _r) for _n in range(2) for s in ("lC%d%d", "sC%d%d")]
for _c in range(3):
    for _i in range(2):
        SCRATCH["dW%d%d" % (_c, _i)] = ("dram", [128, 2 * NC], X4)
        SCRATCH["dV%d%d" % (_c, _i)] = ("dram", [128, 2 * NC], "uint8")
        SEMAPHORES += ["rW%d%d" % (_c, _i), "rV%d%d" % (_c, _i)]
PLANES = ("wp", "wcp", "qp", "dY")
LEFT, RIGHT, THIRD = (0, NC), (NC, 2 * NC), (2 * NC, 3 * NC)


def bits(mask):
    return [b for b in range(16) if mask >> b & 1]


def half(mask):
    b = bits(mask)
    return sum(1 << e for e in b[:len(b) // 2])


def layout(T, topo):
    cores = list(T.cores)
    chips = []
    for c in cores:
        if topo.chip(c) not in chips:
            chips.append(topo.chip(c))
    L = {"chips": chips, "ranks": [[c for c in cores if topo.chip(c) == ch] for ch in chips], "cores": cores}
    far = lambda c: [s for s in cores if topo.chip(s) != topo.chip(c)]
    owns = lambda c: all(topo.may_write(c, s) for s in far(c))
    idle = [[c for c in range(SIM) if topo.chip(c) == ch and c not in cores] for ch in chips]
    L["port"] = [[c for c in m if owns(c)] for m in L["ranks"]]
    L["inner"] = [[c for c in m if not owns(c)] for m in L["ranks"]]
    L["gather"] = [[c for c in m if owns(c)] for m in idle]
    L["scatter"] = [[c for c in m if not owns(c)] for m in idle]
    L["home"] = chips.index(topo.chip(cores[0]))
    L["away"] = [k for k in range(len(chips)) if k != L["home"]]
    L["pair"] = {}
    for p, n in zip(L["port"], L["inner"]):
        for c in p:
            d = [v for v in n if topo.die(v) == topo.die(c)][0]
            L["pair"][c], L["pair"][d] = d, c
    return L


def plan(L, topo):
    prog = {}
    home, away, chips = L["home"], L["away"], L["chips"]
    rank = lambda c: L["cores"].index(c)
    where = lambda c: chips.index(topo.chip(c))

    def wait(c, *sems):
        prog.setdefault(c, []).extend(("wait", s) for s in sems)

    def send(c, ts, local="ls"):
        prog.setdefault(c, []).append(("send", ts, local))

    def onchip(c):
        return topo.mask(c, [s for s in L["ranks"][where(c)] if s != c][0])

    def offchip(c):
        return topo.mask(c, L["ranks"][away[0] if where(c) == home else home][0])

    def piece(kind, i, dsts, mask):
        name = "d%s%s" % (kind, i)
        return (name, None, [(d, name, None) for d in dsts], mask, "r%s%s" % (kind, i))

    def c_out(c):
        ranks = L["ranks"][where(c)]
        k = ranks.index(c)
        col = ((k % 2) * NC, (k % 2) * NC + NC)
        for src, buf, i, kind in (("dX", "wc", "iC", "C%d" % k), ("dY", "wcp", "iD", "P%d" % k)):
            wait(c, i)
            send(c, [(src, None, [(L["gather"][where(c)][k // 2], buf, col)] + [(s, "d" + kind, None) for s in ranks if s != c],
                      onchip(c), "r" + kind)])

    def pass_on(c, cols, dcols, sems, local="ls"):
        for q, r in zip(("q", "qp"), sems):
            send(c, [(q, cols, [(L["pair"][c], q, dcols)], onchip(c), r)], local)

    def x_out(c):
        wait(c, "vq")
        pass_on(c, LEFT, RIGHT, ("rQ", "rR"))

    via = {}
    for c in L["inner"][home]:
        via[c] = []
        for k in away:
            m = [v for v in range(SIM) if topo.mates(topo.chip(v), chips[k]) and topo.die(v) == topo.die(c)
                 and topo.may_write(v, L["port"][k][0])][0]
            via[c].append(m)
            for kind in "BT":
                wait(m, "r%s%d" % (kind, rank(c)))
                send(m, [piece(kind, rank(c), L["port"][k], topo.mask(m, L["port"][k][0]))])

    for k in range(len(chips)):
        ports, inners = L["port"][k], L["inner"][k]
        for c in inners:
            other = [s for s in inners if s != c]
            if k == home:
                i, off, part = rank(c), offchip(c), half(onchip(c))
                for kind in "AZ":
                    wait(c, "i" + kind)
                    send(c, [piece(kind, i, [L["pair"][c]], part)])
                for kind in "AZ":
                    send(c, [piece(kind, i, other, part)])
                for kind in "BT":
                    wait(c, "i" + kind)
                    send(c, [piece(kind, i, via[c], off), piece(kind, i, ports, onchip(c) & ~off)])
                c_out(c)
            else:
                c_out(c)
                e = [v for v in L["port"][home] if topo.die(v) == topo.die(c)][0]
                for kind, buf in (("A", "w"), ("Z", "wp")):
                    name = "%s%d" % (kind, rank(e))
                    wait(c, "r" + name)
                    send(c, [("d" + name, None, [(s, buf, RIGHT) for s in other], onchip(c), "r" + name)])
                for kind in "AZ":
                    wait(c, "r%s%d" % (kind, rank(L["pair"][e])))
                    send(c, [piece(kind, rank(L["pair"][e]), other, onchip(c))])
            wait(c, "v1")
            pass_on(c, THIRD, RIGHT, ("rG", "rH"), "lsG")
            wait(c, "v2")
            pass_on(c, THIRD, THIRD, ("rDG", "rDH"))
        for c in ports:
            if k == home:
                i, l, off = rank(c), rank(L["pair"][c]), offchip(c)
                on = onchip(c) & ~off
                same = lambda group: [s for v in away for s in L[group][v] if topo.die(s) == topo.die(c)]
                for kind in "AZ":
                    wait(c, "i" + kind)
                    send(c, [piece(kind, i, same("inner"), off)])
                for kind in "AZ":
                    send(c, [piece(kind, i, inners, on)])
                x_out(c)
                for kind in "AZ":
                    wait(c, "r%s%d" % (kind, l))
                    send(c, [piece(kind, l, same("inner"), off)])
                for kind in "BT":
                    wait(c, "i" + kind)
                    send(c, [piece(kind, i, same("port"), off), piece(kind, i, [s for s in ports if s != c], on)])
                c_out(c)
            else:
                x_out(c)
                c_out(c)
                e = [v for v in L["port"][home] if topo.die(v) == topo.die(c)][0]
                for kind in "BT":
                    wait(c, "r%s%d" % (kind, rank(e)))
                    send(c, [piece(kind, rank(e), [s for s in ports if s != c], onchip(c))])
            wait(c, "v1", "rDG", "rDH")
            pass_on(c, RIGHT, THIRD, ("rh", "ri"))
        for n in range(2):
            c = L["gather"][k][n]
            for buf, kind, r in (("wc", "W", "rC%d"), ("wcp", "V", "rP%d")):
                name = "%s%d%d" % (kind, k, n)
                wait(c, r % (2 * n), r % (2 * n + 1))
                send(c, [(buf, (0, 2 * NC), [(L["scatter"][v][n], "d" + name, None) for v in range(len(chips)) if v != k],
                          offchip(c), "r" + name)])
            c = L["scatter"][k][n]
            for v in near(L, topo, k):
                for kind in "WV":
                    name = "%d%d" % (v, n)
                    wait(c, "r%s%s" % (kind, name))
                    send(c, [piece(kind, name, L["ranks"][k], onchip(c))])
    return prog


def near(L, topo, k):
    rest = [v for v in range(len(L["chips"])) if v != k]
    return sorted(rest, key=lambda v: 0 if topo.same_plane(L["chips"][v], L["chips"][k]) else 1)


def totals(prog, core):
    n = {}
    for c in prog:
        for op in prog[c]:
            if op[0] == "send":
                for t in op[1]:
                    e = len(bits(t[3]))
                    for d in t[2]:
                        if d[0] == core:
                            n[t[4]] = n.get(t[4], 0) + e
                    if c == core:
                        n[op[2]] = n.get(op[2], 0) + e
    return n


def rank_program(g, core, T, topo):
    L = layout(T, topo)
    prog = plan(L, topo)
    if core not in prog:
        return
    count = totals(prog, core)
    for s in ("iA", "iZ", "iB", "iT", "iC", "iD", "ix"):
        count[s] = 16
    for s in ("vq", "v1", "v2"):
        count[s] = 1
    sem = T.sem

    def wait(q, *names):
        for n in names:
            q.wait_ge(sem[n], count[n])

    def view(name, cols):
        t = T[name]
        v = t[:, 0:t.shape[1]] if cols is None else t[:, cols[0]:cols[1]]
        return v if name in PLANES or name[:2] in ("dZ", "dT", "dV", "dP") else v.bitcast(dt.uint8)

    def remote():
        for op in prog[core]:
            if op[0] == "wait":
                wait(g, op[1])
                continue
            ts = []
            for src, cols, dsts, mask, rsem in op[1]:
                ids = []
                for d in dsts:
                    rid, pid, _s = topo.addr(d[0])
                    ids.append(DstId(rid=rid, pnc=pid))
                ts.append(RemoteDMATransfer(dst_ids=ids, dma_engine_mask=mask, remote_sem=sem[rsem], srcs=[view(src, cols)],
                                            dsts=[view(d[1], d[2]) for d in dsts]))
            g.remote_dma_fused(ts, local_sem=sem[op[2]])
        wait(g, "ls")

    rank = T.rank_of(core)
    if rank is None:
        remote()
        return
    me = L["chips"].index(topo.chip(core))
    first_layer = core in L["inner"][me]

    if me != L["home"]:
        g.sync.dma_start(T.tx[:], T.x[:]).then_inc(sem.ix, 16)
    else:
        g.sync.dma_start(view("dA%d" % rank, None), T.ac[:]).then_inc(sem.iA, 16)
        g.scalar.dma_start(view("dZ%d" % rank, None), T.az[:]).then_inc(sem.iZ, 16)
        g.sync.dma_start(T.tx[:], T.x[:]).then_inc(sem.ix, 16)
        g.scalar.dma_start(view("dB%d" % rank, None), T.bc[:]).then_inc(sem.iB, 16)
        g.sync.dma_start(view("dT%d" % rank, None), T.bs[:]).then_inc(sem.iT, 16)
    g.scalar.dma_start(view("dX", None), T.cc[:]).then_inc(sem.iC, 16)
    g.sync.dma_start(view("dY", None), T.cs[:]).then_inc(sem.iD, 16)

    remote()

    own = lambda c: 0 if topo.die(c) == topo.die(core) else 1
    order = [L["cores"].index(c) for kind in ("port", "inner") for c in sorted(L[kind][L["home"]], key=own)]
    order.sort(key=lambda i: i != rank)
    kind = "AZ" if first_layer else "BT"
    own_in = {"A": T.ac, "Z": T.az, "B": T.bc, "T": T.bs}
    landed = first_layer and me != L["home"]

    def load(q, k, name, after):
        i, s = order[k], RIGHT if k % 2 else LEFT
        if i != rank:
            wait(q, *["r%s%d" % (x, i) for x in kind])
        if after:
            q.wait_ge(sem[after], 1)
        for x, buf in zip(kind, ("w", "wp")):
            src = own_in[x][:] if i == rank else view("d%s%d" % (x, i), None)
            q.dma_start(view(buf, s), src).then_inc(sem[name], 16)

    def product(bank, w, s, cols, done):
        n = cols[1] - cols[0]
        g.tensor.matmul_mx(T.ps[:, 512 * bank:512 * bank + n], T[w][:, s * NC:s * NC + NC], T[w + "p"][:, s * NC:s * NC + NC],
                           T.q[:, cols[0]:cols[1]], T.qp[:, cols[0]:cols[1]], True, True).then_inc(sem[done], 1)

    def result(jobs, e, cols, done):
        for k, col, m in jobs:
            q = g.vector if k % 2 else g.scalar
            q.wait_ge(sem[m % k], 1)
            out, z = T.tg[:, order[k]:G * NC:G], T.ps[:, 512 * k + col:512 * k + col + NC]
            if k % 2:
                r = q.tensor_scalar(out, z, SCALE, 0.0, AluOpType.mult, AluOpType.max)
            else:
                r = q.activation(out, z, ActivationFunctionType.Relu, scale=SCALE)
            r.then_inc(sem[e % k], 1)
        for k in range(G):
            g.vector.wait_ge(sem[e % k], 1)
        if done == "v2" and first_layer:
            wait(g.vector, "lsG")
        g.vector.quantize_mx(T.q[:, cols[0]:cols[1]], T.qp[:, cols[0]:cols[1]], T.tg[:, 0:G * NC]).then_inc(sem[done], 1)
        if done == "v1":
            g.scalar.wait_ge(sem.v1, 1)
            g.vector.wait_ge(sem.v1, 1)

    ranks = L["ranks"]
    a, b = near(L, topo, me)
    lanes = [[(me, 0, 2), (a, 0, 2), (a, 2, 2), (b, 0, 2)], [(me, 2, 1), (me, 3, 1), (b, 2, 1), (b, 3, 1)]]
    span = [(0, 2 * NC), (2 * NC, 3 * NC)]

    def load_c(q, n, r):
        v, i, m = lanes[n][r]
        if v != me:
            name, cols = "%d%d" % (v, i // 2), ((i % 2) * NC, (i % 2 + m) * NC)
            wait(q, "rW" + name, "rV" + name)
            jobs = [(span[n], view("dW" + name, cols), view("dV" + name, cols))]
        else:
            jobs = []
            for h in range(m):
                s, k = (span[n][0] + h * NC, span[n][0] + h * NC + NC), i + h
                if ranks[me][k] == core:
                    jobs.append((s, T.cc[:], T.cs[:]))
                else:
                    wait(q, "rC%d" % k, "rP%d" % k)
                    jobs.append((s, view("dC%d" % k, None), view("dP%d" % k, None)))
        for s, codes, plane in jobs:
            q.dma_start(view("wc", s), codes).then_inc(sem["lC%d%d" % (n, r)], 16)
            q.dma_start(view("wcp", s), plane).then_inc(sem["lC%d%d" % (n, r)], 16)

    g.vector.wait_ge(sem.ix, 16)
    g.vector.quantize_mx(T.q[:, 0:NC], T.qp[:, 0:NC], T.tx[:, 0:G * NC]).then_inc(sem.vq, 1)
    load(g.sync, 0, "lW0", None)
    if not landed:
        load(g.scalar, 1, "lW1", None)
    if first_layer:
        wait(g.tensor, "vq", "rQ", "rR")
    else:
        for n in range(2):
            load_c(g.sync, n, 0)
        wait(g.tensor, "rG", "rH")
    for k in range(G):
        if k == 1 and landed:
            wait(g.tensor, "rA%d" % order[1], "rZ%d" % order[1])
        else:
            g.tensor.wait_ge(sem["lW%d" % k], 32)
        if first_layer:
            cols = LEFT[0], RIGHT[1]
        elif k < 2:
            cols = RIGHT
        else:
            cols = RIGHT[0], THIRD[1]
            wait(g.tensor, "rDG", "rDH")
        product(k, "w", k % 2, cols, "mP%d" % k)
    load(g.sync, 2, "lW2", "mP0")
    load(g.scalar, 3, "lW3", "mP1")
    if first_layer:
        result([(k, 0, "mP%d") for k in range(G)], "aP%d", THIRD, "v1")
        result([(k, NC, "mP%d") for k in range(G)], "aQ%d", THIRD, "v2")
        wait(g.sync, "ls")
        for n in range(2):
            load_c(g.sync, n, 0)
        wait(g.tensor, "rh", "ri")
    else:
        for k in range(2):
            load(g.sync, k, "lV%d" % k, "mP%d" % (k + 2))
            g.tensor.wait_ge(sem["lV%d" % k], 32)
            g.tensor.wait_ge(sem["aP%d" % k], 1)
            product(k, "w", k, THIRD, "mQ%d" % k)
        result([(k, 0, "mP%d") for k in range(G)], "aP%d", RIGHT, "v1")
        result([(2, NC, "mP%d"), (3, NC, "mP%d"), (0, 0, "mQ%d"), (1, 0, "mQ%d")], "aQ%d", THIRD, "v2")
        g.tensor.wait_ge(sem.v2, 1)

    bank = lambda n, r, h: 6 + r % 2 if n else 4 + h
    for r in range(4):
        for n in (1, 0):
            v, i, m = lanes[n][r]
            g.tensor.wait_ge(sem["lC%d%d" % (n, r)], 32 * (m if v == me else 1))
            for h in range(m):
                if r > n:
                    g.tensor.wait_ge(sem["cC%d%d" % (r - 1 - n, 2 * n + h)], 1)
                product(bank(n, r, h), "wc", 2 * n + h, THIRD, "mC%d%d" % (r, 2 * n + h))
    for n, q, cq in ((0, g.sync, g.vector), (1, g.scalar, g.scalar)):
        for r in range(4):
            v, i, m = lanes[n][r]
            for h in range(m):
                q.wait_ge(sem["mC%d%d" % (r, 2 * n + h)], 1)
            if r < 3:
                load_c(q, n, r + 1)
            j = L["cores"].index(ranks[v][i]) * NC
            for h in range(m):
                c = "cC%d%d" % (r, 2 * n + h)
                y, z = T.yb[:, (2 * n + h) * NC:(2 * n + h) * NC + NC], T.ps[:, 512 * bank(n, r, h):512 * bank(n, r, h) + NC]
                cq.wait_ge(sem["mC%d%d" % (r, 2 * n + h)], 1)
                if r and not h:
                    cq.wait_ge(sem["sC%d%d" % (n, r - 1)], 16)
                if n:
                    cq.activation(y, z, ActivationFunctionType.Copy).then_inc(sem[c], 1)
                else:
                    cq.tensor_copy(y, z).then_inc(sem[c], 1)
                q.wait_ge(sem[c], 1)
                if r == 3:
                    q.dma_start(T.y[:, j + h * NC:j + h * NC + NC], y).then_inc(sem["sC%d3" % n], 16)
            if r < 3:
                q.dma_start(T.y[:, j:j + m * NC], T.yb[:, span[n][0]:span[n][1]]).then_inc(sem["sC%d%d" % (n, r)], 16)
        q.wait_ge(sem["sC%d3" % n], 16 * lanes[n][3][2])
